import numpy as np
import ml_dtypes


def mxq(x, axis, fmt="e4m3"):
    dtype, down = {"e4m3": (ml_dtypes.float8_e4m3fn, 7), "e5m2": (ml_dtypes.float8_e5m2, 14)}[fmt]
    v = np.moveaxis(np.asarray(x, np.float32).astype(ml_dtypes.bfloat16).astype(np.float64), axis, -1)
    blocks = v.reshape(v.shape[:-1] + (-1, 32))
    amax = np.abs(blocks).max(-1, keepdims=True)
    byte = np.maximum(np.where(amax > 0, np.frexp(amax)[1] - 1 + 127, 0) - down, 1)
    scale = np.exp2(byte - 127.0)
    codes = (blocks / scale).astype(np.float32).astype(dtype).astype(np.float64)
    return np.moveaxis((codes * scale).reshape(v.shape), -1, axis)


WIDE = False


def mx_kscale(k):
    if not WIDE:
        return np.ones(k)
    levels = np.array([10, -10, 5, -5, 0])
    if k % 512:
        return np.exp2(np.random.permutation(np.resize(levels, k // 32))).repeat(32)
    a = np.empty((k // 512, 16))
    for p in range(k // 512):
        a[p, :8] = np.random.permutation(np.resize(levels, 8))
        for g in range(8):
            far = levels[np.abs(levels - a[p, g]) >= 10]
            a[p, g + 8] = far[np.random.randint(len(far))]
    return np.exp2(a.ravel()).repeat(32)


def f64(x):
    return np.asarray(x).astype(np.float64)


def striped(idx):
    return np.tile(idx.reshape(-1, 16).T, (8, 1)).astype(np.uint16)


def unstriped(offs):
    return offs[:16].T.reshape(-1).astype(np.int64)


E2M1 = np.array([0.0, 0.5, 1.0, 1.5, 2.0, 3.0, 4.0, 6.0, -0.0, -0.5, -1.0, -1.5, -2.0, -3.0, -4.0, -6.0])


def pack_weight(w, fmt):
    k, n = w.shape
    w = f64(np.asarray(w, np.float32).astype(ml_dtypes.bfloat16)).reshape(k // 32, 32, n)
    amax = np.abs(w).max(1)
    if fmt == "e4m3":
        byte = np.frexp(amax)[1] - 1 + 127 - 7
    else:
        mant, ex = np.frexp(amax / 6.0)
        byte = np.where(mant > 0.5, ex, ex - 1) + 127
    byte = np.clip(np.where(amax > 0, byte, 1), 1, 254)
    scaled = (w * np.exp2(127.0 - byte)[:, None, :]).reshape(k, n).astype(np.float32)
    by_word = np.ascontiguousarray(scaled.reshape(k // 512, 128, 4, n).transpose(0, 1, 3, 2))
    if fmt == "e4m3":
        words = by_word.astype(ml_dtypes.float8_e4m3fn).view(np.uint8)
    else:
        c = by_word.astype(ml_dtypes.float4_e2m1fn).view(np.uint8) & 0xF
        words = (c[..., 0::2] | (c[..., 1::2] << 4)).reshape(k // 512, 128, 2 * n)
    return np.ascontiguousarray(words), np.ascontiguousarray(byte.astype(np.uint8).reshape(k // 512, 16, n))


def unpack_weight(words, scales, fmt):
    g, _, n = scales.shape
    words = np.ascontiguousarray(words).reshape(g, 128, n, -1)
    if fmt == "e4m3":
        vals = words.view(ml_dtypes.float8_e4m3fn).astype(np.float64)
    else:
        nib = np.empty((g, 128, n, 4), np.uint8)
        nib[..., 0::2] = words & 0xF
        nib[..., 1::2] = words >> 4
        vals = E2M1[nib]
    vals = vals * np.repeat(np.exp2(scales.astype(np.float64) - 127.0), 8, axis=1)[..., None]
    return vals.transpose(0, 1, 3, 2).reshape(g * 512, n)


def gelu(v):
    return 0.5 * v * (1.0 + np.tanh(np.sqrt(2.0 / np.pi) * (v + 0.044715 * v**3)))


K, T, S, S2, T3, P = 512, 4096, 1024, 1024, 2048, 512


def setup_inputs():
    n = np.random.standard_normal
    s = mx_kscale(K)[:, None]
    u = mx_kscale(K)[:, None]
    d = {}
    d["tab_words"], d["tab_scales"] = pack_weight(n((K, T)) * s, "e4m3")
    d["offs"] = striped(np.random.permutation(T)[:S])
    d["tab2_words"], d["tab2_scales"] = pack_weight(n((K, T3)) / u / K**0.5, "e4m3")
    d["offs2"] = striped(np.random.permutation(T3)[:S2])
    d["pos1"] = striped(np.random.permutation(S)[:P])
    d["pos2"] = striped(np.random.permutation(S)[:P])
    d["w"] = (1.5 * n((K, K)) / s / K**0.5).astype(np.float32)
    d["w4_words"], d["w4_scales"] = pack_weight(0.7 * n((K, K)) / s / K**0.5, "e2m1")
    d["mid"] = (np.exp(0.5 * n(K)) * s[:, 0]).astype(np.float32)
    d["gain"] = (0.19 * np.exp(0.4 * n(K)) * u[:, 0]).astype(np.float32)
    d["fam"] = np.exp(0.4 * n(S2)).astype(np.float32)
    return d


def reference(tab_words, tab_scales, offs, tab2_words, tab2_scales, offs2, pos1, pos2,
              w, w4_words, w4_scales, mid, gain, fam):
    v = unpack_weight(tab_words, tab_scales, "e4m3")[:, unstriped(offs)]
    v2 = unpack_weight(tab2_words, tab2_scales, "e4m3")[:, unstriped(offs2)]
    wq = mxq(f64(w), 0, "e4m3")
    w4 = unpack_weight(w4_words, w4_scales, "e2m1")
    x = np.tanh(wq.T @ v) * f64(mid)[:, None]
    xq = mxq(x, 0, "e4m3")
    h = (wq.T @ xq + w4.T @ v) * f64(gain)[:, None]
    e = v2.T @ mxq(h, 0, "e4m3")
    diff = e[:, unstriped(pos1)] - e[:, unstriped(pos2)]
    return np.cos(diff) * f64(fam)[:, None]

@@ -1,0 +1,215 @@
+import math
+from contextlib import ExitStack
+
+import concourse.mybir as mybir
+
+K, T, S, S2, T3, PAIRS = 512, 4096, 1024, 1024, 2048, 512
+FLOPS = 2 * K * K * S * 3 + 2 * K * S2 * S
+
+F32 = mybir.dt.float32
+BF16 = mybir.dt.bfloat16
+I32 = mybir.dt.int32
+U32 = mybir.dt.uint32
+U16 = mybir.dt.uint16
+U8 = mybir.dt.uint8
+FP8X4 = mybir.dt.float8_e4m3fn_x4
+FP4X4 = mybir.dt.float4_e2m1fn_x4
+ALU = mybir.AluOpType
+ACT = mybir.ActivationFunctionType
+
+P = 128
+PACK = 4
+CHUNK = 256
+BANK = 512
+
+
+def load_scale_rows(queue, plane, scales):
+    for q in range(4):
+        queue.dma_start(out=plane[32 * q : 32 * q + 4, :].bitcast(I32), in_=scales[0, 4 * q : 4 * q + 4, :].bitcast(I32))
+
+
+def tile_list_glitch_pair_cosine_kernel(tc, tab_words, tab_scales, offs, tab2_words, tab2_scales, offs2, pos1, pos2,
+                                                 w, w4_words, w4_scales, mid, gain, fam, out):
+    nc = tc.nc
+    with ExitStack() as ctx:
+        keep = ctx.enter_context(tc.tile_pool(name="keep", bufs=1))
+        ring = ctx.enter_context(tc.tile_pool(name="ring", bufs=3))
+        psum = ctx.enter_context(tc.psum_pool(name="psum", bufs=8))
+
+        offs_t = keep.tile([P, S // 16], U16)
+        offs2_t = keep.tile([P, S2 // 16], U16)
+        pos1_t = keep.tile([P, PAIRS // 16], U16)
+        pos2_t = keep.tile([P, PAIRS // 16], U16)
+        tab_w = keep.tile([P, T], U32, tag="table", align_bytes=64)
+        tab_s = keep.tile([P, T], U8, tag="rows", align_bytes=64)
+        tab2_s = keep.tile([P, T3], U8, tag="rows2", align_bytes=64)
+        w4_raw = keep.tile([P, 2 * K], U8, tag="small", align_bytes=64)
+        w_raw = keep.tile([P, PACK * K], F32, tag="big", align_bytes=64)
+        mid_t = keep.tile([P, PACK], F32)
+        gain_t = keep.tile([P, PACK], F32)
+
+        w4_s_raw = keep.tile([P, K], U8, align_bytes=64)
+        nc.vector.memset(tab_s[:].bitcast(I32), 0)
+        nc.vector.memset(tab2_s[:].bitcast(I32), 0)
+        nc.vector.memset(w4_s_raw[:].bitcast(I32), 0)
+
+        nc.sync.dma_start(offs_t[:], offs)
+        load_scale_rows(nc.sync, tab_s, tab_scales)
+        nc.sync.dma_start(offs2_t[:], offs2)
+        nc.sync.dma_start(pos1_t[:], pos1)
+        nc.sync.dma_start(pos2_t[:], pos2)
+        nc.sync.dma_start(out=mid_t[:], in_=mid.rearrange("(p t) -> p t", t=PACK))
+        nc.sync.dma_start(out=gain_t[:], in_=gain.rearrange("(p t) -> p t", t=PACK))
+        nc.sync.dma_start(out=w4_raw[:].bitcast(I32), in_=w4_words[0].bitcast(I32))
+        nc.sync.dma_start(out=w_raw[:], in_=w.rearrange("(p j) c -> p (j c)", j=PACK))
+        nc.sync.dma_start(out=tab_w[:].bitcast(I32), in_=tab_words[0].rearrange("p t i -> p (t i)").bitcast(I32))
+        load_scale_rows(nc.scalar, tab2_s, tab2_scales)
+        load_scale_rows(nc.sync, w4_s_raw, w4_scales)
+
+        v_s = keep.tile([P, S], U8, align_bytes=64)
+        nc.vector.tensor_copy(v_s[:], tab_s[:].indirect(offs_t[:]))
+
+        w_bf = keep.tile([P, K * PACK], BF16, align_bytes=64)
+        nc.scalar.copy(out=w_bf[:].rearrange("p (t m j) -> p m t j", t=PACK, j=PACK),
+                       in_=w_raw[:].rearrange("p (j m t) -> p m t j", j=PACK, t=PACK))
+        tab2_w = keep.tile([P, T3], U32, tag="big", align_bytes=64)
+        nc.sync.dma_start(out=tab2_w[:].bitcast(I32), in_=tab2_words[0].rearrange("p t i -> p (t i)").bitcast(I32))
+
+        v2_s = keep.tile([P, S2], U8, tag="rows", align_bytes=64)
+        nc.vector.tensor_copy(v2_s[:], tab2_s[:].indirect(offs2_t[:]))
+
+        w_c = keep.tile([P, K], U32, align_bytes=64)
+        w_s = keep.tile([P, K], U8, align_bytes=64)
+        nc.vector.quantize_mx(out=w_c[:].bitcast(FP8X4), scales=w_s[:], in_=w_bf[:])
+
+        v_w = [keep.tile([P, BANK], U32, name=f"v_w{h}", tag=("rows2", "v_w1")[h], align_bytes=64) for h in range(S // BANK)]
+        for h in range(S // BANK):
+            nc.vector.tensor_copy(v_w[h][:], tab_w[:].indirect(offs_t[:, h * BANK // 16 : (h + 1) * BANK // 16]))
+
+        w4_c = keep.tile([P, 2 * K], U8, tag="table", align_bytes=64)
+        w4_s = keep.tile([P, K], U8, align_bytes=64)
+        nc.vector.tensor_copy(out=w4_c[:].rearrange("p (t m b) -> p m t b", t=PACK, b=2),
+                              in_=w4_raw[:].rearrange("p (m t b) -> p m t b", t=PACK, b=2))
+        nc.vector.tensor_copy(out=w4_s[:].rearrange("p (t m) -> p m t", t=PACK),
+                              in_=w4_s_raw[:].rearrange("p (m t) -> p m t", t=PACK))
+        fam_t = keep.tile([P, S2 // P], F32, tag="small", align_bytes=64)
+        with nc.allow_non_contiguous_dma(reason="one value of fam for each output row"):
+            nc.sync.dma_start(out=fam_t[:], in_=fam.rearrange("(i p) -> p i", p=P))
+
+        def v_cols(j0, n):
+            return v_w[j0 // BANK][:, j0 % BANK : j0 % BANK + n].bitcast(FP8X4), v_s[:, j0 : j0 + n]
+
+        x_c = keep.tile([P, S], U32, align_bytes=64)
+        x_s = keep.tile([P, S], U8, align_bytes=64)
+        h_c = keep.tile([P, S], U32, align_bytes=64)
+        h_s = keep.tile([P, S], U8, align_bytes=64)
+        v2_w = {}
+
+        def stage1(c):
+            bent = ring.tile([P, CHUNK, PACK], F32, tag="bent")
+            for b in range(CHUNK // P):
+                bank = psum.tile([P, PACK, P], F32, tag="bank")
+                rhs, rhs_s = v_cols(c * CHUNK + b * P, P)
+                for t in range(PACK):
+                    nc.tensor.matmul_mx(out=bank[:, t, :], lhsT=w_c[:, t * P : (t + 1) * P].bitcast(FP8X4),
+                                        lhsT_scale=w_s[:, t * P : (t + 1) * P], rhs=rhs, rhs_scale=rhs_s, start=True, stop=True)
+                nc.scalar.activation(out=bent[:, b * P : (b + 1) * P, :], in_=bank[:].rearrange("p t n -> p n t"), func=ACT.Tanh)
+            x_bf = ring.tile([P, CHUNK, PACK], BF16, tag="x_bf", align_bytes=64)
+            nc.vector.tensor_tensor(out=x_bf[:], in0=bent[:], in1=mid_t[:].unsqueeze(1).to_broadcast([P, CHUNK, PACK]), op=ALU.mult)
+            return x_bf
+
+        def quantize(codes, scales, c, values):
+            cols = slice(c * CHUNK, (c + 1) * CHUNK)
+            nc.vector.quantize_mx(out=codes[:, cols].bitcast(FP8X4), scales=scales[:, cols], in_=values[:].rearrange("p n t -> p (n t)"))
+
+        def stage2(c):
+            planes = ring.tile([P, PACK, CHUNK], BF16, tag="planes")
+            for u in range(PACK // 2):
+                bank = psum.tile([P, 2, CHUNK], F32, tag="bank")
+                for e in range(2):
+                    t = 2 * u + e
+                    for b in range(CHUNK // P):
+                        j0 = c * CHUNK + b * P
+                        rhs, rhs_s = v_cols(j0, P)
+                        acc = bank[:, e, b * P : (b + 1) * P]
+                        nc.tensor.matmul_mx(out=acc, lhsT=w4_c[:, 2 * t * P : 2 * (t + 1) * P].bitcast(FP4X4),
+                                            lhsT_scale=w4_s[:, t * P : (t + 1) * P], rhs=rhs, rhs_scale=rhs_s, start=True, stop=False)
+                        nc.tensor.matmul_mx(out=acc, lhsT=w_c[:, t * P : (t + 1) * P].bitcast(FP8X4),
+                                            lhsT_scale=w_s[:, t * P : (t + 1) * P], rhs=x_c[:, j0 : j0 + P].bitcast(FP8X4),
+                                            rhs_scale=x_s[:, j0 : j0 + P], start=False, stop=True)
+                for e in range(2):
+                    t = 2 * u + e
+                    nc.scalar.activation(out=planes[:, t, :], in_=bank[:, e, :], func=ACT.Copy, scale=gain_t[:, t : t + 1])
+            return planes
+
+        def weave(c, planes):
+            h_bf = keep.tile([P, CHUNK, PACK], BF16, tag=f"h_bf{c}", align_bytes=64)
+            nc.vector.tensor_copy(out=h_bf[:].rearrange("p (c i) t -> p c t i", i=4), in_=planes[:].rearrange("p t (c i) -> p c t i", i=4))
+            return h_bf
+
+        def gather_families(c):
+            v2_w[c] = keep.tile([P, CHUNK], U32, name=f"v2_w{c}", tag=f"h_bf{c}" if c == S2 // CHUNK - 1 else f"v2_w{c}", align_bytes=64)
+            nc.vector.tensor_copy(v2_w[c][:], tab2_w[:].indirect(offs2_t[:, c * CHUNK // 16 : (c + 1) * CHUNK // 16]))
+
+        tiles = S2 // P
+        scores = [keep.tile([P, S], F32, name=f"scores{i}") for i in range(tiles)]
+
+        def stage3(i, j0, n):
+            cols = slice(j0, j0 + n)
+            m0 = i * P % CHUNK
+            bank = psum.tile([P, BANK], F32, tag="bank")
+            nc.tensor.matmul_mx(out=bank[:, :n], lhsT=v2_w[i * P // CHUNK][:, m0 : m0 + P].bitcast(FP8X4), lhsT_scale=v2_s[:, i * P : (i + 1) * P],
+                                rhs=h_c[:, cols].bitcast(FP8X4), rhs_scale=h_s[:, cols], start=True, stop=True)
+            nc.scalar.copy(out=scores[i][:, cols], in_=bank[:, :n])
+
+        chunks = S // CHUNK
+        xs, hs = {}, {}
+        for step in range(chunks + 2):
+            if step < chunks:
+                xs[step] = stage1(step)
+            if 0 <= step - 2 < chunks:
+                hs[step - 2] = weave(step - 2, hs[step - 2])
+            if step < chunks:
+                quantize(x_c, x_s, step, xs[step])
+            if 0 <= step - 2 < chunks:
+                quantize(h_c, h_s, step - 2, hs[step - 2])
+            if 0 <= step - 1 < chunks:
+                hs[step - 1] = stage2(step - 1)
+            if step >= 2:
+                gather_families(step - 2)
+            if step == chunks:
+                stage3(0, 0, BANK)
+                stage3(0, BANK, CHUNK)
+                stage3(1, 0, BANK)
+        stage3(0, BANK + CHUNK, CHUNK)
+        stage3(1, BANK, BANK)
+        for i in range(2, tiles):
+            for h in range(S // BANK):
+                stage3(i, h * BANK, BANK)
+
+        pieces = [(i, 0, PAIRS) for i in range(tiles - 1)] + [(tiles - 1, 0, PAIRS // 2), (tiles - 1, PAIRS // 2, PAIRS // 2)]
+        second, diff, turns = {}, {}, {}
+        for step in range(len(pieces) + 1):
+            last = step - 1
+            if step < len(pieces):
+                i, j0, n = pieces[step]
+                entries = slice(j0 // 16, (j0 + n) // 16)
+                second[step] = ring.tile([P, n], F32, tag="second", name="second")
+                nc.vector.tensor_copy(second[step][:], scores[i][:].indirect(pos2_t[:, entries]))
+            if last >= 0:
+                li, lj0, ln = pieces[last]
+                turns[last] = ring.tile([P, ln], I32, tag="turns", name="turns")
+                nc.vector.tensor_scalar(out=turns[last][:], in0=diff[last][:], scalar1=1.0 / (2.0 * math.pi), scalar2=0.25,
+                                        op0=ALU.mult, op1=ALU.add)
+            if step < len(pieces):
+                diff[step] = ring.tile([P, n], F32, tag="diff", name="diff")
+                nc.vector.tensor_tensor(out=diff[step][:], in0=scores[i][:].indirect(pos1_t[:, entries]), in1=second[step][:], op=ALU.subtract)
+            if last >= 0:
+                angle = ring.tile([P, ln], F32, tag="angle", bufs=5)
+                nc.vector.scalar_tensor_tensor(out=angle[:], in0=turns[last][:], scalar=-2.0 * math.pi, in1=diff[last][:],
+                                               op0=ALU.mult, op1=ALU.add)
+                wave = ring.tile([P, ln], F32, tag="wave")
+                nc.scalar.activation(out=wave[:], in_=angle[:], func=ACT.Sin, bias=math.pi / 2.0)
+                result = ring.tile([P, ln], F32, tag="result")
+                nc.scalar.activation(out=result[:], in_=wave[:], func=ACT.Copy, scale=fam_t[:, li : li + 1])
+                nc.sync.dma_start(out=out[li * P : (li + 1) * P, lj0 : lj0 + ln], in_=result[:])

@@ -23,8 +23,8 @@ CHUNK = 256
 BANK = 512
 
 
-def load_scale_rows(queue, plane, scales):
-    for q in range(4):
+def load_scale_rows(queues, plane, scales):
+    for q, queue in enumerate(queues):
         queue.dma_start(out=plane[32 * q : 32 * q + 4, :].bitcast(I32), in_=scales[0, 4 * q : 4 * q + 4, :].bitcast(I32))
 
 
@@ -48,56 +48,58 @@ def tile_list_glitch_pair_cosine_kernel(tc, tab_words, tab_scales, offs, tab2_wo
         mid_t = keep.tile([P, PACK], F32)
         gain_t = keep.tile([P, PACK], F32)
 
-        w4_s_raw = keep.tile([P, K], U8, align_bytes=64)
         nc.vector.memset(tab_s[:].bitcast(I32), 0)
         nc.vector.memset(tab2_s[:].bitcast(I32), 0)
-        nc.vector.memset(w4_s_raw[:].bitcast(I32), 0)
 
         nc.sync.dma_start(offs_t[:], offs)
-        load_scale_rows(nc.sync, tab_s, tab_scales)
         nc.sync.dma_start(offs2_t[:], offs2)
         nc.sync.dma_start(pos1_t[:], pos1)
         nc.sync.dma_start(pos2_t[:], pos2)
-        nc.sync.dma_start(out=mid_t[:], in_=mid.rearrange("(p t) -> p t", t=PACK))
-        nc.sync.dma_start(out=gain_t[:], in_=gain.rearrange("(p t) -> p t", t=PACK))
-        nc.sync.dma_start(out=w4_raw[:].bitcast(I32), in_=w4_words[0].bitcast(I32))
+        load_scale_rows([nc.scalar] * 4, tab_s, tab_scales)
         nc.sync.dma_start(out=w_raw[:], in_=w.rearrange("(p j) c -> p (j c)", j=PACK))
         nc.sync.dma_start(out=tab_w[:].bitcast(I32), in_=tab_words[0].rearrange("p t i -> p (t i)").bitcast(I32))
-        load_scale_rows(nc.scalar, tab2_s, tab2_scales)
-        load_scale_rows(nc.sync, w4_s_raw, w4_scales)
+        load_scale_rows([nc.scalar] * 3 + [nc.gpsimd], tab2_s, tab2_scales)
+        nc.gpsimd.dma_start(out=mid_t[:], in_=mid.rearrange("(p t) -> p t", t=PACK))
+        nc.gpsimd.dma_start(out=w4_raw[:].bitcast(I32), in_=w4_words[0].bitcast(I32))
+        nc.gpsimd.dma_start(out=gain_t[:], in_=gain.rearrange("(p t) -> p t", t=PACK))
 
         v_s = keep.tile([P, S], U8, align_bytes=64)
         nc.vector.tensor_copy(v_s[:], tab_s[:].indirect(offs_t[:]))
 
+        w4_s_raw = keep.tile([P, K], U8, tag="rows", align_bytes=64)
+        nc.vector.memset(w4_s_raw[:].bitcast(I32), 0)
+        load_scale_rows([nc.sync] * 4, w4_s_raw, w4_scales)
+
         w_bf = keep.tile([P, K * PACK], BF16, align_bytes=64)
         nc.scalar.copy(out=w_bf[:].rearrange("p (t m j) -> p m t j", t=PACK, j=PACK),
                        in_=w_raw[:].rearrange("p (j m t) -> p m t j", j=PACK, t=PACK))
-        tab2_w = keep.tile([P, T3], U32, tag="big", align_bytes=64)
-        nc.sync.dma_start(out=tab2_w[:].bitcast(I32), in_=tab2_words[0].rearrange("p t i -> p (t i)").bitcast(I32))
 
-        v2_s = keep.tile([P, S2], U8, tag="rows", align_bytes=64)
+        v2_s = keep.tile([P, S2], U8, align_bytes=64)
         nc.vector.tensor_copy(v2_s[:], tab2_s[:].indirect(offs2_t[:]))
 
         w_c = keep.tile([P, K], U32, align_bytes=64)
         w_s = keep.tile([P, K], U8, align_bytes=64)
         nc.vector.quantize_mx(out=w_c[:].bitcast(FP8X4), scales=w_s[:], in_=w_bf[:])
 
-        v_w = [keep.tile([P, BANK], U32, name=f"v_w{h}", tag=("rows2", "v_w1")[h], align_bytes=64) for h in range(S // BANK)]
+        tab2_w = keep.tile([P, T3], U32, tag="big", align_bytes=64)
+        nc.sync.dma_start(out=tab2_w[:].bitcast(I32), in_=tab2_words[0].rearrange("p t i -> p (t i)").bitcast(I32))
+
+        v_w = keep.tile([P, S], U32, tag="rows2", align_bytes=64)
         for h in range(S // BANK):
-            nc.vector.tensor_copy(v_w[h][:], tab_w[:].indirect(offs_t[:, h * BANK // 16 : (h + 1) * BANK // 16]))
+            nc.vector.tensor_copy(v_w[:, h * BANK : (h + 1) * BANK], tab_w[:].indirect(offs_t[:, h * BANK // 16 : (h + 1) * BANK // 16]))
 
         w4_c = keep.tile([P, 2 * K], U8, tag="table", align_bytes=64)
-        w4_s = keep.tile([P, K], U8, align_bytes=64)
         nc.vector.tensor_copy(out=w4_c[:].rearrange("p (t m b) -> p m t b", t=PACK, b=2),
                               in_=w4_raw[:].rearrange("p (m t b) -> p m t b", t=PACK, b=2))
+        w4_s = keep.tile([P, K], U8, tag="small", align_bytes=64)
         nc.vector.tensor_copy(out=w4_s[:].rearrange("p (t m) -> p m t", t=PACK),
                               in_=w4_s_raw[:].rearrange("p (m t) -> p m t", t=PACK))
-        fam_t = keep.tile([P, S2 // P], F32, tag="small", align_bytes=64)
+        fam_t = keep.tile([P, S2 // P], F32, tag="rows", align_bytes=64)
         with nc.allow_non_contiguous_dma(reason="one value of fam for each output row"):
             nc.sync.dma_start(out=fam_t[:], in_=fam.rearrange("(i p) -> p i", p=P))
 
         def v_cols(j0, n):
-            return v_w[j0 // BANK][:, j0 % BANK : j0 % BANK + n].bitcast(FP8X4), v_s[:, j0 : j0 + n]
+            return v_w[:, j0 : j0 + n].bitcast(FP8X4), v_s[:, j0 : j0 + n]
 
         x_c = keep.tile([P, S], U32, align_bytes=64)
         x_s = keep.tile([P, S], U8, align_bytes=64)
@@ -106,7 +108,7 @@ def tile_list_glitch_pair_cosine_kernel(tc, tab_words, tab_scales, offs, tab2_wo
         v2_w = {}
 
         def stage1(c):
-            bent = ring.tile([P, CHUNK, PACK], F32, tag="bent")
+            bent = ring.tile([P, CHUNK, PACK], F32, tag="bent", bufs=4)
             for b in range(CHUNK // P):
                 bank = psum.tile([P, PACK, P], F32, tag="bank")
                 rhs, rhs_s = v_cols(c * CHUNK + b * P, P)
@@ -123,20 +125,22 @@ def tile_list_glitch_pair_cosine_kernel(tc, tab_words, tab_scales, offs, tab2_wo
             nc.vector.quantize_mx(out=codes[:, cols].bitcast(FP8X4), scales=scales[:, cols], in_=values[:].rearrange("p n t -> p (n t)"))
 
         def stage2(c):
-            planes = ring.tile([P, PACK, CHUNK], BF16, tag="planes")
+            planes = ring.tile([P, PACK, CHUNK], BF16, tag="planes", bufs=4)
             for u in range(PACK // 2):
                 bank = psum.tile([P, 2, CHUNK], F32, tag="bank")
                 for e in range(2):
                     t = 2 * u + e
                     for b in range(CHUNK // P):
-                        j0 = c * CHUNK + b * P
-                        rhs, rhs_s = v_cols(j0, P)
-                        acc = bank[:, e, b * P : (b + 1) * P]
-                        nc.tensor.matmul_mx(out=acc, lhsT=w4_c[:, 2 * t * P : 2 * (t + 1) * P].bitcast(FP4X4),
-                                            lhsT_scale=w4_s[:, t * P : (t + 1) * P], rhs=rhs, rhs_scale=rhs_s, start=True, stop=False)
-                        nc.tensor.matmul_mx(out=acc, lhsT=w_c[:, t * P : (t + 1) * P].bitcast(FP8X4),
-                                            lhsT_scale=w_s[:, t * P : (t + 1) * P], rhs=x_c[:, j0 : j0 + P].bitcast(FP8X4),
-                                            rhs_scale=x_s[:, j0 : j0 + P], start=False, stop=True)
+                        rhs, rhs_s = v_cols(c * CHUNK + b * P, P)
+                        nc.tensor.matmul_mx(out=bank[:, e, b * P : (b + 1) * P], lhsT=w4_c[:, 2 * t * P : 2 * (t + 1) * P].bitcast(FP4X4),
+                                            lhsT_scale=w4_s[:, t * P : (t + 1) * P], rhs=rhs, rhs_scale=rhs_s,
+                                            start=(e == 0 and b == 0), stop=False)
+                cols = slice(c * CHUNK, (c + 1) * CHUNK)
+                for e in range(2):
+                    t = 2 * u + e
+                    nc.tensor.matmul_mx(out=bank[:, e, :], lhsT=w_c[:, t * P : (t + 1) * P].bitcast(FP8X4),
+                                        lhsT_scale=w_s[:, t * P : (t + 1) * P], rhs=x_c[:, cols].bitcast(FP8X4),
+                                        rhs_scale=x_s[:, cols], start=False, stop=(e == 1))
                 for e in range(2):
                     t = 2 * u + e
                     nc.scalar.activation(out=planes[:, t, :], in_=bank[:, e, :], func=ACT.Copy, scale=gain_t[:, t : t + 1])
@@ -144,11 +148,11 @@ def tile_list_glitch_pair_cosine_kernel(tc, tab_words, tab_scales, offs, tab2_wo
 
         def weave(c, planes):
             h_bf = keep.tile([P, CHUNK, PACK], BF16, tag=f"h_bf{c}", align_bytes=64)
-            nc.vector.tensor_copy(out=h_bf[:].rearrange("p (c i) t -> p c t i", i=4), in_=planes[:].rearrange("p t (c i) -> p c t i", i=4))
+            nc.vector.tensor_copy(out=h_bf[:], in_=planes[:].rearrange("p t n -> p n t"))
             return h_bf
 
         def gather_families(c):
-            v2_w[c] = keep.tile([P, CHUNK], U32, name=f"v2_w{c}", tag=f"h_bf{c}" if c == S2 // CHUNK - 1 else f"v2_w{c}", align_bytes=64)
+            v2_w[c] = keep.tile([P, CHUNK], U32, name=f"v2_w{c}", tag=f"h_bf{c}" if c > 0 else f"v2_w{c}", align_bytes=64)
             nc.vector.tensor_copy(v2_w[c][:], tab2_w[:].indirect(offs2_t[:, c * CHUNK // 16 : (c + 1) * CHUNK // 16]))
 
         tiles = S2 // P
@@ -164,52 +168,57 @@ def tile_list_glitch_pair_cosine_kernel(tc, tab_words, tab_scales, offs, tab2_wo
 
         chunks = S // CHUNK
         xs, hs = {}, {}
-        for step in range(chunks + 2):
+        for step in range(chunks + 1):
             if step < chunks:
                 xs[step] = stage1(step)
-            if 0 <= step - 2 < chunks:
-                hs[step - 2] = weave(step - 2, hs[step - 2])
+            if step >= 1:
+                quantize(x_c, x_s, step - 1, xs[step - 1])
+        gather_families(0)
+        for step in range(chunks + 1):
             if step < chunks:
-                quantize(x_c, x_s, step, xs[step])
-            if 0 <= step - 2 < chunks:
-                quantize(h_c, h_s, step - 2, hs[step - 2])
-            if 0 <= step - 1 < chunks:
-                hs[step - 1] = stage2(step - 1)
-            if step >= 2:
-                gather_families(step - 2)
-            if step == chunks:
+                hs[step] = weave(step, stage2(step))
+            if step >= 1:
+                quantize(h_c, h_s, step - 1, hs[step - 1])
+            if step == chunks - 1:
                 stage3(0, 0, BANK)
                 stage3(0, BANK, CHUNK)
                 stage3(1, 0, BANK)
+        for c in range(1, S2 // CHUNK):
+            gather_families(c)
         stage3(0, BANK + CHUNK, CHUNK)
         stage3(1, BANK, BANK)
         for i in range(2, tiles):
             for h in range(S // BANK):
                 stage3(i, h * BANK, BANK)
 
-        pieces = [(i, 0, PAIRS) for i in range(tiles - 1)] + [(tiles - 1, 0, PAIRS // 2), (tiles - 1, PAIRS // 2, PAIRS // 2)]
+        pieces = [(i, 0, PAIRS) for i in range(tiles - 1)] + [(tiles - 1, 0, PAIRS - P), (tiles - 1, PAIRS - P, P)]
         second, diff, turns = {}, {}, {}
         for step in range(len(pieces) + 1):
             last = step - 1
             if step < len(pieces):
                 i, j0, n = pieces[step]
                 entries = slice(j0 // 16, (j0 + n) // 16)
-                second[step] = ring.tile([P, n], F32, tag="second", name="second")
+                second[step] = ring.tile([P, n], F32, tag="held" if step == len(pieces) - 1 else "second", name="second",
+                                         bufs=1 if step == len(pieces) - 1 else 3)
                 nc.vector.tensor_copy(second[step][:], scores[i][:].indirect(pos2_t[:, entries]))
             if last >= 0:
                 li, lj0, ln = pieces[last]
-                turns[last] = ring.tile([P, ln], I32, tag="turns", name="turns")
+                turns[last] = ring.tile([P, ln], I32, tag="held" if last == len(pieces) - 3 else "turns", name="turns",
+                                        bufs=1 if last == len(pieces) - 3 else 3)
                 nc.vector.tensor_scalar(out=turns[last][:], in0=diff[last][:], scalar1=1.0 / (2.0 * math.pi), scalar2=0.25,
                                         op0=ALU.mult, op1=ALU.add)
             if step < len(pieces):
-                diff[step] = ring.tile([P, n], F32, tag="diff", name="diff")
+                diff[step] = ring.tile([P, n], F32, tag="diff", name="diff", bufs=2)
                 nc.vector.tensor_tensor(out=diff[step][:], in0=scores[i][:].indirect(pos1_t[:, entries]), in1=second[step][:], op=ALU.subtract)
             if last >= 0:
-                angle = ring.tile([P, ln], F32, tag="angle", bufs=5)
+                angle = ring.tile([P, ln], F32, tag="angle", bufs=9)
                 nc.vector.scalar_tensor_tensor(out=angle[:], in0=turns[last][:], scalar=-2.0 * math.pi, in1=diff[last][:],
                                                op0=ALU.mult, op1=ALU.add)
                 wave = ring.tile([P, ln], F32, tag="wave")
                 nc.scalar.activation(out=wave[:], in_=angle[:], func=ACT.Sin, bias=math.pi / 2.0)
-                result = ring.tile([P, ln], F32, tag="result")
-                nc.scalar.activation(out=result[:], in_=wave[:], func=ACT.Copy, scale=fam_t[:, li : li + 1])
+                result = ring.tile([P, ln], F32, tag="result", bufs=9)
+                if li < tiles - 1:
+                    nc.scalar.activation(out=result[:], in_=wave[:], func=ACT.Copy, scale=fam_t[:, li : li + 1])
+                else:
+                    nc.vector.tensor_scalar_mul(out=result[:], in0=wave[:], scalar1=fam_t[:, li : li + 1])
                 nc.sync.dma_start(out=out[li * P : (li + 1) * P, lj0 : lj0 + ln], in_=result[:])

@@ -43,28 +43,43 @@ def tile_list_glitch_pair_cosine_kernel(tc, tab_words, tab_scales, offs, tab2_wo
         tab_w = keep.tile([P, T], U32, tag="table", align_bytes=64)
         tab_s = keep.tile([P, T], U8, tag="rows", align_bytes=64)
         tab2_s = keep.tile([P, T3], U8, tag="rows2", align_bytes=64)
-        w4_raw = keep.tile([P, 2 * K], U8, tag="small", align_bytes=64)
+        w4_raw = keep.tile([P, 2 * K], U8, align_bytes=64)
         w_raw = keep.tile([P, PACK * K], F32, tag="big", align_bytes=64)
         mid_t = keep.tile([P, PACK], F32)
-        gain_t = keep.tile([P, PACK], F32)
 
+        v_s = keep.tile([P, S], U8, align_bytes=64)
+        v2_s = keep.tile([P, S2], U8, align_bytes=64)
+        warm = keep.tile([P, 1], F32)
+        nc.gpsimd.memset(warm[:], 0.0)
         nc.vector.memset(tab_s[:].bitcast(I32), 0)
         nc.vector.memset(tab2_s[:].bitcast(I32), 0)
+        nc.vector.memset(v_s[:].bitcast(I32), 0)
+        nc.vector.memset(v2_s[:].bitcast(I32), 0)
 
         nc.sync.dma_start(offs_t[:], offs)
         nc.sync.dma_start(offs2_t[:], offs2)
         nc.sync.dma_start(pos1_t[:], pos1)
         nc.sync.dma_start(pos2_t[:], pos2)
-        load_scale_rows([nc.scalar] * 4, tab_s, tab_scales)
-        nc.sync.dma_start(out=w_raw[:], in_=w.rearrange("(p j) c -> p (j c)", j=PACK))
-        nc.sync.dma_start(out=tab_w[:].bitcast(I32), in_=tab_words[0].rearrange("p t i -> p (t i)").bitcast(I32))
-        load_scale_rows([nc.scalar] * 3 + [nc.gpsimd], tab2_s, tab2_scales)
-        nc.gpsimd.dma_start(out=mid_t[:], in_=mid.rearrange("(p t) -> p t", t=PACK))
-        nc.gpsimd.dma_start(out=w4_raw[:].bitcast(I32), in_=w4_words[0].bitcast(I32))
-        nc.gpsimd.dma_start(out=gain_t[:], in_=gain.rearrange("(p t) -> p t", t=PACK))
+        nc.sync.dma_start(out=w4_raw[:].bitcast(I32), in_=w4_words[0].bitcast(I32))
+        nc.scalar.dma_start(out=mid_t[:], in_=mid.rearrange("(p t) -> p t", t=PACK))
+        nc.scalar.dma_start(out=w_raw[:], in_=w.rearrange("(p j) c -> p (j c)", j=PACK))
+        warmed = keep.tile([P, 1], F32)
+        nc.scalar.activation(out=warmed[:], in_=warm[:], func=ACT.Silu)
+        nc.sync.dma_start(out=tab_s[0:P:8, :].bitcast(I32), in_=tab_scales[0].bitcast(I32))
+        nc.scalar.dma_start(out=tab2_s[0:P:8, :].bitcast(I32), in_=tab2_scales[0].bitcast(I32))
+        nc.scalar.dma_start(out=tab_w[:].bitcast(I32), in_=tab_words[0].rearrange("p t i -> p (t i)").bitcast(I32))
 
-        v_s = keep.tile([P, S], U8, align_bytes=64)
-        nc.vector.tensor_copy(v_s[:], tab_s[:].indirect(offs_t[:]))
+        w4_c = keep.tile([P, 2 * K], U8, align_bytes=64)
+        nc.vector.tensor_copy(out=w4_c[:].rearrange("p (t m b) -> p m t b", t=PACK, b=2),
+                              in_=w4_raw[:].rearrange("p (m t b) -> p m t b", t=PACK, b=2))
+
+        def place_scale_rows(plane, picked):
+            for q in range(4):
+                nc.sync.dma_start(out=plane[32 * q : 32 * q + 4, :].bitcast(I32), in_=picked[32 * q : 32 * q + 32 : 8, :].bitcast(I32))
+
+        v_picked = keep.tile([P, S], U8, tag="picked", align_bytes=64)
+        nc.vector.tensor_copy(v_picked[:], tab_s[:].indirect(offs_t[:]))
+        place_scale_rows(v_s, v_picked)
 
         w4_s_raw = keep.tile([P, K], U8, tag="rows", align_bytes=64)
         nc.vector.memset(w4_s_raw[:].bitcast(I32), 0)
@@ -74,8 +89,9 @@ def tile_list_glitch_pair_cosine_kernel(tc, tab_words, tab_scales, offs, tab2_wo
         nc.scalar.copy(out=w_bf[:].rearrange("p (t m j) -> p m t j", t=PACK, j=PACK),
                        in_=w_raw[:].rearrange("p (j m t) -> p m t j", j=PACK, t=PACK))
 
-        v2_s = keep.tile([P, S2], U8, align_bytes=64)
-        nc.vector.tensor_copy(v2_s[:], tab2_s[:].indirect(offs2_t[:]))
+        v2_picked = keep.tile([P, S2], U8, align_bytes=64)
+        nc.vector.tensor_copy(v2_picked[:], tab2_s[:].indirect(offs2_t[:]))
+        place_scale_rows(v2_s, v2_picked)
 
         w_c = keep.tile([P, K], U32, align_bytes=64)
         w_s = keep.tile([P, K], U8, align_bytes=64)
@@ -88,10 +104,9 @@ def tile_list_glitch_pair_cosine_kernel(tc, tab_words, tab_scales, offs, tab2_wo
         for h in range(S // BANK):
             nc.vector.tensor_copy(v_w[:, h * BANK : (h + 1) * BANK], tab_w[:].indirect(offs_t[:, h * BANK // 16 : (h + 1) * BANK // 16]))
 
-        w4_c = keep.tile([P, 2 * K], U8, tag="table", align_bytes=64)
-        nc.vector.tensor_copy(out=w4_c[:].rearrange("p (t m b) -> p m t b", t=PACK, b=2),
-                              in_=w4_raw[:].rearrange("p (m t b) -> p m t b", t=PACK, b=2))
-        w4_s = keep.tile([P, K], U8, tag="small", align_bytes=64)
+        gain_t = keep.tile([P, PACK], F32, tag="picked", align_bytes=64)
+        nc.sync.dma_start(out=gain_t[:], in_=gain.rearrange("(p t) -> p t", t=PACK))
+        w4_s = keep.tile([P, K], U8, tag="table", align_bytes=64)
         nc.vector.tensor_copy(out=w4_s[:].rearrange("p (t m) -> p m t", t=PACK),
                               in_=w4_s_raw[:].rearrange("p (m t) -> p m t", t=PACK))
         fam_t = keep.tile([P, S2 // P], F32, tag="rows", align_bytes=64)
@@ -118,6 +133,23 @@ def tile_list_glitch_pair_cosine_kernel(tc, tab_words, tab_scales, offs, tab2_wo
                 nc.scalar.activation(out=bent[:, b * P : (b + 1) * P, :], in_=bank[:].rearrange("p t n -> p n t"), func=ACT.Tanh)
             x_bf = ring.tile([P, CHUNK, PACK], BF16, tag="x_bf", align_bytes=64)
             nc.vector.tensor_tensor(out=x_bf[:], in0=bent[:], in1=mid_t[:].unsqueeze(1).to_broadcast([P, CHUNK, PACK]), op=ALU.mult)
+            return x_bf
+
+        def stage1_scaled_on_scalar(c):
+            bent = ring.tile([P, PACK, CHUNK], F32, tag="bent", bufs=4)
+            planes = ring.tile([P, PACK, CHUNK], BF16, tag="planes", bufs=4)
+            rhs, rhs_s = v_cols(c * CHUNK, CHUNK)
+            for u in range(PACK // 2):
+                bank = psum.tile([P, 2, CHUNK], F32, tag="bank")
+                for e in range(2):
+                    t = 2 * u + e
+                    nc.tensor.matmul_mx(out=bank[:, e, :], lhsT=w_c[:, t * P : (t + 1) * P].bitcast(FP8X4),
+                                        lhsT_scale=w_s[:, t * P : (t + 1) * P], rhs=rhs, rhs_scale=rhs_s, start=True, stop=True)
+                nc.scalar.activation(out=bent[:, 2 * u : 2 * u + 2, :], in_=bank[:], func=ACT.Tanh)
+            for t in range(PACK):
+                nc.scalar.activation(out=planes[:, t, :], in_=bent[:, t, :], func=ACT.Copy, scale=mid_t[:, t : t + 1])
+            x_bf = ring.tile([P, CHUNK, PACK], BF16, tag="x_bf", align_bytes=64)
+            nc.vector.tensor_copy(out=x_bf[:], in_=planes[:].rearrange("p t n -> p n t"))
             return x_bf
 
         def quantize(codes, scales, c, values):
@@ -170,7 +202,7 @@ def tile_list_glitch_pair_cosine_kernel(tc, tab_words, tab_scales, offs, tab2_wo
         xs, hs = {}, {}
         for step in range(chunks + 1):
             if step < chunks:
-                xs[step] = stage1(step)
+                xs[step] = stage1(step) if step < chunks - 1 else stage1_scaled_on_scalar(step)
             if step >= 1:
                 quantize(x_c, x_s, step - 1, xs[step - 1])
         gather_families(0)
@@ -192,7 +224,23 @@ def tile_list_glitch_pair_cosine_kernel(tc, tab_words, tab_scales, offs, tab2_wo
                 stage3(i, h * BANK, BANK)
 
         pieces = [(i, 0, PAIRS) for i in range(tiles - 1)] + [(tiles - 1, 0, PAIRS - P), (tiles - 1, PAIRS - P, P)]
+        on_scalar = (2, 3, 4)
         second, diff, turns = {}, {}, {}
+
+        def finish(last):
+            li, lj0, ln = pieces[last]
+            angle = ring.tile([P, ln], F32, tag="angle", bufs=9)
+            nc.vector.scalar_tensor_tensor(out=angle[:], in0=turns[last][:].bitcast(I32), scalar=-2.0 * math.pi, in1=diff[last][:],
+                                           op0=ALU.mult, op1=ALU.add)
+            wave = ring.tile([P, ln], F32, tag="wave")
+            nc.scalar.activation(out=wave[:], in_=angle[:], func=ACT.Sin, bias=math.pi / 2.0)
+            result = ring.tile([P, ln], F32, tag="result", bufs=9)
+            if li < tiles - 1:
+                nc.scalar.activation(out=result[:], in_=wave[:], func=ACT.Copy, scale=fam_t[:, li : li + 1])
+            else:
+                nc.vector.tensor_scalar_mul(out=result[:], in0=wave[:], scalar1=fam_t[:, li : li + 1])
+            nc.sync.dma_start(out=out[li * P : (li + 1) * P, lj0 : lj0 + ln], in_=result[:])
+
         for step in range(len(pieces) + 1):
             last = step - 1
             if step < len(pieces):
@@ -201,8 +249,10 @@ def tile_list_glitch_pair_cosine_kernel(tc, tab_words, tab_scales, offs, tab2_wo
                 second[step] = ring.tile([P, n], F32, tag="held" if step == len(pieces) - 1 else "second", name="second",
                                          bufs=1 if step == len(pieces) - 1 else 3)
                 nc.vector.tensor_copy(second[step][:], scores[i][:].indirect(pos2_t[:, entries]))
-            if last >= 0:
-                li, lj0, ln = pieces[last]
+            if step - 2 in on_scalar:
+                finish(step - 2)
+            if last >= 0 and last not in on_scalar:
+                ln = pieces[last][2]
                 turns[last] = ring.tile([P, ln], I32, tag="held" if last == len(pieces) - 3 else "turns", name="turns",
                                         bufs=1 if last == len(pieces) - 3 else 3)
                 nc.vector.tensor_scalar(out=turns[last][:], in0=diff[last][:], scalar1=1.0 / (2.0 * math.pi), scalar2=0.25,
@@ -210,15 +260,11 @@ def tile_list_glitch_pair_cosine_kernel(tc, tab_words, tab_scales, offs, tab2_wo
             if step < len(pieces):
                 diff[step] = ring.tile([P, n], F32, tag="diff", name="diff", bufs=2)
                 nc.vector.tensor_tensor(out=diff[step][:], in0=scores[i][:].indirect(pos1_t[:, entries]), in1=second[step][:], op=ALU.subtract)
-            if last >= 0:
-                angle = ring.tile([P, ln], F32, tag="angle", bufs=9)
-                nc.vector.scalar_tensor_tensor(out=angle[:], in0=turns[last][:], scalar=-2.0 * math.pi, in1=diff[last][:],
-                                               op0=ALU.mult, op1=ALU.add)
-                wave = ring.tile([P, ln], F32, tag="wave")
-                nc.scalar.activation(out=wave[:], in_=angle[:], func=ACT.Sin, bias=math.pi / 2.0)
-                result = ring.tile([P, ln], F32, tag="result", bufs=9)
-                if li < tiles - 1:
-                    nc.scalar.activation(out=result[:], in_=wave[:], func=ACT.Copy, scale=fam_t[:, li : li + 1])
-                else:
-                    nc.vector.tensor_scalar_mul(out=result[:], in0=wave[:], scalar1=fam_t[:, li : li + 1])
-                nc.sync.dma_start(out=out[li * P : (li + 1) * P, lj0 : lj0 + ln], in_=result[:])
+            if step in on_scalar:
+                size = ring.tile([P, n], F32, tag="size")
+                nc.scalar.activation(out=size[:], in_=diff[step][:], func=ACT.Abs)
+                turns[step] = ring.tile([P, n], U32, tag="turns", name="turns")
+                nc.scalar.activation(out=turns[step][:], in_=size[:], func=ACT.Copy, scale=1.0 / (2.0 * math.pi), bias=0.25)
+                diff[step] = size
+            if last >= 0 and last not in on_scalar:
+                finish(last)

@@ -131,25 +131,8 @@ def tile_list_glitch_pair_cosine_kernel(tc, tab_words, tab_scales, offs, tab2_wo
                     nc.tensor.matmul_mx(out=bank[:, t, :], lhsT=w_c[:, t * P : (t + 1) * P].bitcast(FP8X4),
                                         lhsT_scale=w_s[:, t * P : (t + 1) * P], rhs=rhs, rhs_scale=rhs_s, start=True, stop=True)
                 nc.scalar.activation(out=bent[:, b * P : (b + 1) * P, :], in_=bank[:].rearrange("p t n -> p n t"), func=ACT.Tanh)
-            x_bf = ring.tile([P, CHUNK, PACK], BF16, tag="x_bf", align_bytes=64)
+            x_bf = ring.tile([P, CHUNK, PACK], BF16, tag="x_bf", bufs=2, align_bytes=64)
             nc.vector.tensor_tensor(out=x_bf[:], in0=bent[:], in1=mid_t[:].unsqueeze(1).to_broadcast([P, CHUNK, PACK]), op=ALU.mult)
-            return x_bf
-
-        def stage1_scaled_on_scalar(c):
-            bent = ring.tile([P, PACK, CHUNK], F32, tag="bent", bufs=4)
-            planes = ring.tile([P, PACK, CHUNK], BF16, tag="planes", bufs=4)
-            rhs, rhs_s = v_cols(c * CHUNK, CHUNK)
-            for u in range(PACK // 2):
-                bank = psum.tile([P, 2, CHUNK], F32, tag="bank")
-                for e in range(2):
-                    t = 2 * u + e
-                    nc.tensor.matmul_mx(out=bank[:, e, :], lhsT=w_c[:, t * P : (t + 1) * P].bitcast(FP8X4),
-                                        lhsT_scale=w_s[:, t * P : (t + 1) * P], rhs=rhs, rhs_scale=rhs_s, start=True, stop=True)
-                nc.scalar.activation(out=bent[:, 2 * u : 2 * u + 2, :], in_=bank[:], func=ACT.Tanh)
-            for t in range(PACK):
-                nc.scalar.activation(out=planes[:, t, :], in_=bent[:, t, :], func=ACT.Copy, scale=mid_t[:, t : t + 1])
-            x_bf = ring.tile([P, CHUNK, PACK], BF16, tag="x_bf", align_bytes=64)
-            nc.vector.tensor_copy(out=x_bf[:], in_=planes[:].rearrange("p t n -> p n t"))
             return x_bf
 
         def quantize(codes, scales, c, values):
@@ -178,6 +161,23 @@ def tile_list_glitch_pair_cosine_kernel(tc, tab_words, tab_scales, offs, tab2_wo
                     nc.scalar.activation(out=planes[:, t, :], in_=bank[:, e, :], func=ACT.Copy, scale=gain_t[:, t : t + 1])
             return planes
 
+        def stage2_on_vector(c):
+            h_bf = keep.tile([P, CHUNK, PACK], BF16, tag=f"h_bf{c}", align_bytes=64)
+            for b in range(CHUNK // P):
+                j0 = c * CHUNK + b * P
+                bank = psum.tile([P, PACK, P], F32, tag="bank")
+                rhs, rhs_s = v_cols(j0, P)
+                for t in range(PACK):
+                    nc.tensor.matmul_mx(out=bank[:, t, :], lhsT=w4_c[:, 2 * t * P : 2 * (t + 1) * P].bitcast(FP4X4),
+                                        lhsT_scale=w4_s[:, t * P : (t + 1) * P], rhs=rhs, rhs_scale=rhs_s, start=(t == 0), stop=False)
+                for t in range(PACK):
+                    nc.tensor.matmul_mx(out=bank[:, t, :], lhsT=w_c[:, t * P : (t + 1) * P].bitcast(FP8X4),
+                                        lhsT_scale=w_s[:, t * P : (t + 1) * P], rhs=x_c[:, j0 : j0 + P].bitcast(FP8X4),
+                                        rhs_scale=x_s[:, j0 : j0 + P], start=False, stop=(t == PACK - 1))
+                nc.vector.tensor_tensor(out=h_bf[:, b * P : (b + 1) * P, :], in0=bank[:].rearrange("p t n -> p n t"),
+                                        in1=gain_t[:].unsqueeze(1).to_broadcast([P, P, PACK]), op=ALU.mult)
+            return h_bf
+
         def weave(c, planes):
             h_bf = keep.tile([P, CHUNK, PACK], BF16, tag=f"h_bf{c}", align_bytes=64)
             nc.vector.tensor_copy(out=h_bf[:], in_=planes[:].rearrange("p t n -> p n t"))
@@ -202,13 +202,13 @@ def tile_list_glitch_pair_cosine_kernel(tc, tab_words, tab_scales, offs, tab2_wo
         xs, hs = {}, {}
         for step in range(chunks + 1):
             if step < chunks:
-                xs[step] = stage1(step) if step < chunks - 1 else stage1_scaled_on_scalar(step)
+                xs[step] = stage1(step)
             if step >= 1:
                 quantize(x_c, x_s, step - 1, xs[step - 1])
         gather_families(0)
         for step in range(chunks + 1):
             if step < chunks:
-                hs[step] = weave(step, stage2(step))
+                hs[step] = weave(step, stage2(step)) if step < chunks - 1 else stage2_on_vector(step)
             if step >= 1:
                 quantize(h_c, h_s, step - 1, hs[step - 1])
             if step == chunks - 1:
@@ -219,17 +219,17 @@ def tile_list_glitch_pair_cosine_kernel(tc, tab_words, tab_scales, offs, tab2_wo
             gather_families(c)
         stage3(0, BANK + CHUNK, CHUNK)
         stage3(1, BANK, BANK)
-        for i in range(2, tiles):
-            for h in range(S // BANK):
-                stage3(i, h * BANK, BANK)
+        ahead = 3
+        for h in range(S // BANK):
+            stage3(2, h * BANK, BANK)
 
-        pieces = [(i, 0, PAIRS) for i in range(tiles - 1)] + [(tiles - 1, 0, PAIRS - P), (tiles - 1, PAIRS - P, P)]
-        on_scalar = (2, 3, 4)
+        pieces = [(i, 0, PAIRS) for i in range(tiles - 1)] + [(tiles - 1, 0, PAIRS // 2), (tiles - 1, PAIRS // 2, PAIRS // 2)]
+        on_scalar = range(1, tiles - 1, 2)
         second, diff, turns = {}, {}, {}
 
         def finish(last):
             li, lj0, ln = pieces[last]
-            angle = ring.tile([P, ln], F32, tag="angle", bufs=9)
+            angle = ring.tile([P, ln], F32, tag="angle", bufs=2)
             nc.vector.scalar_tensor_tensor(out=angle[:], in0=turns[last][:].bitcast(I32), scalar=-2.0 * math.pi, in1=diff[last][:],
                                            op0=ALU.mult, op1=ALU.add)
             wave = ring.tile([P, ln], F32, tag="wave")
@@ -243,28 +243,27 @@ def tile_list_glitch_pair_cosine_kernel(tc, tab_words, tab_scales, offs, tab2_wo
 
         for step in range(len(pieces) + 1):
             last = step - 1
+            if step + ahead < tiles:
+                for h in range(S // BANK):
+                    stage3(step + ahead, h * BANK, BANK)
             if step < len(pieces):
                 i, j0, n = pieces[step]
                 entries = slice(j0 // 16, (j0 + n) // 16)
-                second[step] = ring.tile([P, n], F32, tag="held" if step == len(pieces) - 1 else "second", name="second",
-                                         bufs=1 if step == len(pieces) - 1 else 3)
+                second[step] = ring.tile([P, n], F32, tag="second", name="second")
                 nc.vector.tensor_copy(second[step][:], scores[i][:].indirect(pos2_t[:, entries]))
             if step - 2 in on_scalar:
                 finish(step - 2)
             if last >= 0 and last not in on_scalar:
                 ln = pieces[last][2]
-                turns[last] = ring.tile([P, ln], I32, tag="held" if last == len(pieces) - 3 else "turns", name="turns",
-                                        bufs=1 if last == len(pieces) - 3 else 3)
+                turns[last] = ring.tile([P, ln], I32, tag="turns", name="turns")
                 nc.vector.tensor_scalar(out=turns[last][:], in0=diff[last][:], scalar1=1.0 / (2.0 * math.pi), scalar2=0.25,
                                         op0=ALU.mult, op1=ALU.add)
             if step < len(pieces):
                 diff[step] = ring.tile([P, n], F32, tag="diff", name="diff", bufs=2)
                 nc.vector.tensor_tensor(out=diff[step][:], in0=scores[i][:].indirect(pos1_t[:, entries]), in1=second[step][:], op=ALU.subtract)
             if step in on_scalar:
-                size = ring.tile([P, n], F32, tag="size")
-                nc.scalar.activation(out=size[:], in_=diff[step][:], func=ACT.Abs)
+                nc.scalar.activation(out=diff[step][:], in_=diff[step][:], func=ACT.Abs)
                 turns[step] = ring.tile([P, n], U32, tag="turns", name="turns")
-                nc.scalar.activation(out=turns[step][:], in_=size[:], func=ACT.Copy, scale=1.0 / (2.0 * math.pi), bias=0.25)
-                diff[step] = size
+                nc.scalar.activation(out=turns[step][:], in_=diff[step][:], func=ACT.Copy, scale=1.0 / (2.0 * math.pi), bias=0.25)
             if last >= 0 and last not in on_scalar:
                 finish(last)

import math
from contextlib import ExitStack

import concourse.mybir as mybir

K, T, S, S2, T3, PAIRS = 512, 4096, 1024, 1024, 2048, 512
FLOPS = 2 * K * K * S * 3 + 2 * K * S2 * S

F32 = mybir.dt.float32
BF16 = mybir.dt.bfloat16
I32 = mybir.dt.int32
U32 = mybir.dt.uint32
U16 = mybir.dt.uint16
U8 = mybir.dt.uint8
FP8X4 = mybir.dt.float8_e4m3fn_x4
FP4X4 = mybir.dt.float4_e2m1fn_x4
ALU = mybir.AluOpType
ACT = mybir.ActivationFunctionType

P = 128
PACK = 4
CHUNK = 256
BANK = 512


def load_scale_rows(queues, plane, scales):
    for q, queue in enumerate(queues):
        queue.dma_start(out=plane[32 * q : 32 * q + 4, :].bitcast(I32), in_=scales[0, 4 * q : 4 * q + 4, :].bitcast(I32))


def tile_list_glitch_pair_cosine_kernel(tc, tab_words, tab_scales, offs, tab2_words, tab2_scales, offs2, pos1, pos2,
                                                 w, w4_words, w4_scales, mid, gain, fam, out):
    nc = tc.nc
    with ExitStack() as ctx:
        keep = ctx.enter_context(tc.tile_pool(name="keep", bufs=1))
        ring = ctx.enter_context(tc.tile_pool(name="ring", bufs=3))
        psum = ctx.enter_context(tc.psum_pool(name="psum", bufs=8))

        offs_t = keep.tile([P, S // 16], U16)
        offs2_t = keep.tile([P, S2 // 16], U16)
        pos1_t = keep.tile([P, PAIRS // 16], U16)
        pos2_t = keep.tile([P, PAIRS // 16], U16)
        tab_w = keep.tile([P, T], U32, tag="table", align_bytes=64)
        tab_s = keep.tile([P, T], U8, tag="rows", align_bytes=64)
        tab2_s = keep.tile([P, T3], U8, tag="rows2", align_bytes=64)
        w4_raw = keep.tile([P, 2 * K], U8, align_bytes=64)
        w_raw = keep.tile([P, PACK * K], F32, tag="big", align_bytes=64)
        mid_t = keep.tile([P, PACK], F32)

        v_s = keep.tile([P, S], U8, align_bytes=64)
        v2_s = keep.tile([P, S2], U8, align_bytes=64)
        warm = keep.tile([P, 1], F32)
        nc.gpsimd.memset(warm[:], 0.0)
        nc.vector.memset(tab_s[:].bitcast(I32), 0)
        nc.vector.memset(tab2_s[:].bitcast(I32), 0)
        nc.vector.memset(v_s[:].bitcast(I32), 0)
        nc.vector.memset(v2_s[:].bitcast(I32), 0)

        nc.sync.dma_start(offs_t[:], offs)
        nc.sync.dma_start(offs2_t[:], offs2)
        nc.sync.dma_start(pos1_t[:], pos1)
        nc.sync.dma_start(pos2_t[:], pos2)
        nc.sync.dma_start(out=w4_raw[:].bitcast(I32), in_=w4_words[0].bitcast(I32))
        nc.scalar.dma_start(out=mid_t[:], in_=mid.rearrange("(p t) -> p t", t=PACK))
        nc.scalar.dma_start(out=w_raw[:], in_=w.rearrange("(p j) c -> p (j c)", j=PACK))
        warmed = keep.tile([P, 1], F32)
        nc.scalar.activation(out=warmed[:], in_=warm[:], func=ACT.Silu)
        nc.sync.dma_start(out=tab_s[0:P:8, :].bitcast(I32), in_=tab_scales[0].bitcast(I32))
        nc.scalar.dma_start(out=tab2_s[0:P:8, :].bitcast(I32), in_=tab2_scales[0].bitcast(I32))
        nc.scalar.dma_start(out=tab_w[:].bitcast(I32), in_=tab_words[0].rearrange("p t i -> p (t i)").bitcast(I32))

        w4_c = keep.tile([P, 2 * K], U8, align_bytes=64)
        nc.vector.tensor_copy(out=w4_c[:].rearrange("p (t m b) -> p m t b", t=PACK, b=2),
                              in_=w4_raw[:].rearrange("p (m t b) -> p m t b", t=PACK, b=2))

        def place_scale_rows(plane, picked):
            for q in range(4):
                nc.sync.dma_start(out=plane[32 * q : 32 * q + 4, :].bitcast(I32), in_=picked[32 * q : 32 * q + 32 : 8, :].bitcast(I32))

        v_picked = keep.tile([P, S], U8, tag="picked", align_bytes=64)
        nc.vector.tensor_copy(v_picked[:], tab_s[:].indirect(offs_t[:]))
        place_scale_rows(v_s, v_picked)

        w4_s_raw = keep.tile([P, K], U8, tag="rows", align_bytes=64)
        nc.vector.memset(w4_s_raw[:].bitcast(I32), 0)
        load_scale_rows([nc.sync] * 4, w4_s_raw, w4_scales)

        w_bf = keep.tile([P, K * PACK], BF16, align_bytes=64)
        nc.scalar.copy(out=w_bf[:].rearrange("p (t m j) -> p m t j", t=PACK, j=PACK),
                       in_=w_raw[:].rearrange("p (j m t) -> p m t j", j=PACK, t=PACK))

        v2_picked = keep.tile([P, S2], U8, align_bytes=64)
        nc.vector.tensor_copy(v2_picked[:], tab2_s[:].indirect(offs2_t[:]))
        place_scale_rows(v2_s, v2_picked)

        w_c = keep.tile([P, K], U32, align_bytes=64)
        w_s = keep.tile([P, K], U8, align_bytes=64)
        nc.vector.quantize_mx(out=w_c[:].bitcast(FP8X4), scales=w_s[:], in_=w_bf[:])

        tab2_w = keep.tile([P, T3], U32, tag="big", align_bytes=64)
        nc.sync.dma_start(out=tab2_w[:].bitcast(I32), in_=tab2_words[0].rearrange("p t i -> p (t i)").bitcast(I32))

        v_w = keep.tile([P, S], U32, tag="rows2", align_bytes=64)
        for h in range(S // BANK):
            nc.vector.tensor_copy(v_w[:, h * BANK : (h + 1) * BANK], tab_w[:].indirect(offs_t[:, h * BANK // 16 : (h + 1) * BANK // 16]))

        gain_t = keep.tile([P, PACK], F32, tag="picked", align_bytes=64)
        nc.sync.dma_start(out=gain_t[:], in_=gain.rearrange("(p t) -> p t", t=PACK))
        w4_s = keep.tile([P, K], U8, tag="table", align_bytes=64)
        nc.vector.tensor_copy(out=w4_s[:].rearrange("p (t m) -> p m t", t=PACK),
                              in_=w4_s_raw[:].rearrange("p (m t) -> p m t", t=PACK))
        fam_t = keep.tile([P, S2 // P], F32, tag="rows", align_bytes=64)
        with nc.allow_non_contiguous_dma(reason="one value of fam for each output row"):
            nc.sync.dma_start(out=fam_t[:], in_=fam.rearrange("(i p) -> p i", p=P))

        def v_cols(j0, n):
            return v_w[:, j0 : j0 + n].bitcast(FP8X4), v_s[:, j0 : j0 + n]

        x_c = keep.tile([P, S], U32, align_bytes=64)
        x_s = keep.tile([P, S], U8, align_bytes=64)
        h_c = keep.tile([P, S], U32, align_bytes=64)
        h_s = keep.tile([P, S], U8, align_bytes=64)
        v2_w = {}

        def stage1(c):
            bent = ring.tile([P, CHUNK, PACK], F32, tag="bent", bufs=4)
            for b in range(CHUNK // P):
                bank = psum.tile([P, PACK, P], F32, tag="bank")
                rhs, rhs_s = v_cols(c * CHUNK + b * P, P)
                for t in range(PACK):
                    nc.tensor.matmul_mx(out=bank[:, t, :], lhsT=w_c[:, t * P : (t + 1) * P].bitcast(FP8X4),
                                        lhsT_scale=w_s[:, t * P : (t + 1) * P], rhs=rhs, rhs_scale=rhs_s, start=True, stop=True)
                nc.scalar.activation(out=bent[:, b * P : (b + 1) * P, :], in_=bank[:].rearrange("p t n -> p n t"), func=ACT.Tanh)
            x_bf = ring.tile([P, CHUNK, PACK], BF16, tag="x_bf", bufs=2, align_bytes=64)
            nc.vector.tensor_tensor(out=x_bf[:], in0=bent[:], in1=mid_t[:].unsqueeze(1).to_broadcast([P, CHUNK, PACK]), op=ALU.mult)
            return x_bf

        def quantize(codes, scales, c, values):
            cols = slice(c * CHUNK, (c + 1) * CHUNK)
            nc.vector.quantize_mx(out=codes[:, cols].bitcast(FP8X4), scales=scales[:, cols], in_=values[:].rearrange("p n t -> p (n t)"))

        def stage2(c):
            planes = ring.tile([P, PACK, CHUNK], BF16, tag="planes", bufs=4)
            for u in range(PACK // 2):
                bank = psum.tile([P, 2, CHUNK], F32, tag="bank")
                for e in range(2):
                    t = 2 * u + e
                    for b in range(CHUNK // P):
                        rhs, rhs_s = v_cols(c * CHUNK + b * P, P)
                        nc.tensor.matmul_mx(out=bank[:, e, b * P : (b + 1) * P], lhsT=w4_c[:, 2 * t * P : 2 * (t + 1) * P].bitcast(FP4X4),
                                            lhsT_scale=w4_s[:, t * P : (t + 1) * P], rhs=rhs, rhs_scale=rhs_s,
                                            start=(e == 0 and b == 0), stop=False)
                cols = slice(c * CHUNK, (c + 1) * CHUNK)
                for e in range(2):
                    t = 2 * u + e
                    nc.tensor.matmul_mx(out=bank[:, e, :], lhsT=w_c[:, t * P : (t + 1) * P].bitcast(FP8X4),
                                        lhsT_scale=w_s[:, t * P : (t + 1) * P], rhs=x_c[:, cols].bitcast(FP8X4),
                                        rhs_scale=x_s[:, cols], start=False, stop=(e == 1))
                for e in range(2):
                    t = 2 * u + e
                    nc.scalar.activation(out=planes[:, t, :], in_=bank[:, e, :], func=ACT.Copy, scale=gain_t[:, t : t + 1])
            return planes

        def stage2_on_vector(c):
            h_bf = keep.tile([P, CHUNK, PACK], BF16, tag=f"h_bf{c}", align_bytes=64)
            for b in range(CHUNK // P):
                j0 = c * CHUNK + b * P
                bank = psum.tile([P, PACK, P], F32, tag="bank")
                rhs, rhs_s = v_cols(j0, P)
                for t in range(PACK):
                    nc.tensor.matmul_mx(out=bank[:, t, :], lhsT=w4_c[:, 2 * t * P : 2 * (t + 1) * P].bitcast(FP4X4),
                                        lhsT_scale=w4_s[:, t * P : (t + 1) * P], rhs=rhs, rhs_scale=rhs_s, start=(t == 0), stop=False)
                for t in range(PACK):
                    nc.tensor.matmul_mx(out=bank[:, t, :], lhsT=w_c[:, t * P : (t + 1) * P].bitcast(FP8X4),
                                        lhsT_scale=w_s[:, t * P : (t + 1) * P], rhs=x_c[:, j0 : j0 + P].bitcast(FP8X4),
                                        rhs_scale=x_s[:, j0 : j0 + P], start=False, stop=(t == PACK - 1))
                nc.vector.tensor_tensor(out=h_bf[:, b * P : (b + 1) * P, :], in0=bank[:].rearrange("p t n -> p n t"),
                                        in1=gain_t[:].unsqueeze(1).to_broadcast([P, P, PACK]), op=ALU.mult)
            return h_bf

        def weave(c, planes):
            h_bf = keep.tile([P, CHUNK, PACK], BF16, tag=f"h_bf{c}", align_bytes=64)
            nc.vector.tensor_copy(out=h_bf[:], in_=planes[:].rearrange("p t n -> p n t"))
            return h_bf

        def gather_families(c):
            v2_w[c] = keep.tile([P, CHUNK], U32, name=f"v2_w{c}", tag=f"h_bf{c}" if c > 0 else f"v2_w{c}", align_bytes=64)
            nc.vector.tensor_copy(v2_w[c][:], tab2_w[:].indirect(offs2_t[:, c * CHUNK // 16 : (c + 1) * CHUNK // 16]))

        tiles = S2 // P
        scores = [keep.tile([P, S], F32, name=f"scores{i}") for i in range(tiles)]

        def stage3(i, j0, n):
            cols = slice(j0, j0 + n)
            m0 = i * P % CHUNK
            bank = psum.tile([P, BANK], F32, tag="bank")
            nc.tensor.matmul_mx(out=bank[:, :n], lhsT=v2_w[i * P // CHUNK][:, m0 : m0 + P].bitcast(FP8X4), lhsT_scale=v2_s[:, i * P : (i + 1) * P],
                                rhs=h_c[:, cols].bitcast(FP8X4), rhs_scale=h_s[:, cols], start=True, stop=True)
            nc.scalar.copy(out=scores[i][:, cols], in_=bank[:, :n])

        chunks = S // CHUNK
        xs, hs = {}, {}
        for step in range(chunks + 1):
            if step < chunks:
                xs[step] = stage1(step)
            if step >= 1:
                quantize(x_c, x_s, step - 1, xs[step - 1])
        gather_families(0)
        for step in range(chunks + 1):
            if step < chunks:
                hs[step] = weave(step, stage2(step)) if step < chunks - 1 else stage2_on_vector(step)
            if step >= 1:
                quantize(h_c, h_s, step - 1, hs[step - 1])
            if step == chunks - 1:
                stage3(0, 0, BANK)
                stage3(0, BANK, CHUNK)
                stage3(1, 0, BANK)
        for c in range(1, S2 // CHUNK):
            gather_families(c)
        stage3(0, BANK + CHUNK, CHUNK)
        stage3(1, BANK, BANK)
        ahead = 3
        for h in range(S // BANK):
            stage3(2, h * BANK, BANK)

        pieces = [(i, 0, PAIRS) for i in range(tiles - 1)] + [(tiles - 1, 0, PAIRS // 2), (tiles - 1, PAIRS // 2, PAIRS // 2)]
        on_scalar = range(1, tiles - 1, 2)
        second, diff, turns = {}, {}, {}

        def finish(last):
            li, lj0, ln = pieces[last]
            angle = ring.tile([P, ln], F32, tag="angle", bufs=2)
            nc.vector.scalar_tensor_tensor(out=angle[:], in0=turns[last][:].bitcast(I32), scalar=-2.0 * math.pi, in1=diff[last][:],
                                           op0=ALU.mult, op1=ALU.add)
            wave = ring.tile([P, ln], F32, tag="wave")
            nc.scalar.activation(out=wave[:], in_=angle[:], func=ACT.Sin, bias=math.pi / 2.0)
            result = ring.tile([P, ln], F32, tag="result", bufs=9)
            if li < tiles - 1:
                nc.scalar.activation(out=result[:], in_=wave[:], func=ACT.Copy, scale=fam_t[:, li : li + 1])
            else:
                nc.vector.tensor_scalar_mul(out=result[:], in0=wave[:], scalar1=fam_t[:, li : li + 1])
            nc.sync.dma_start(out=out[li * P : (li + 1) * P, lj0 : lj0 + ln], in_=result[:])

        for step in range(len(pieces) + 1):
            last = step - 1
            if step + ahead < tiles:
                for h in range(S // BANK):
                    stage3(step + ahead, h * BANK, BANK)
            if step < len(pieces):
                i, j0, n = pieces[step]
                entries = slice(j0 // 16, (j0 + n) // 16)
                second[step] = ring.tile([P, n], F32, tag="second", name="second")
                nc.vector.tensor_copy(second[step][:], scores[i][:].indirect(pos2_t[:, entries]))
            if step - 2 in on_scalar:
                finish(step - 2)
            if last >= 0 and last not in on_scalar:
                ln = pieces[last][2]
                turns[last] = ring.tile([P, ln], I32, tag="turns", name="turns")
                nc.vector.tensor_scalar(out=turns[last][:], in0=diff[last][:], scalar1=1.0 / (2.0 * math.pi), scalar2=0.25,
                                        op0=ALU.mult, op1=ALU.add)
            if step < len(pieces):
                diff[step] = ring.tile([P, n], F32, tag="diff", name="diff", bufs=2)
                nc.vector.tensor_tensor(out=diff[step][:], in0=scores[i][:].indirect(pos1_t[:, entries]), in1=second[step][:], op=ALU.subtract)
            if step in on_scalar:
                nc.scalar.activation(out=diff[step][:], in_=diff[step][:], func=ACT.Abs)
                turns[step] = ring.tile([P, n], U32, tag="turns", name="turns")
                nc.scalar.activation(out=turns[step][:], in_=diff[step][:], func=ACT.Copy, scale=1.0 / (2.0 * math.pi), bias=0.25)
            if last >= 0 and last not in on_scalar:
                finish(last)
